import numpy as np
import ml_dtypes


def mxq(x, axis, fmt="e4m3"):
    dtype, down = {"e4m3": (ml_dtypes.float8_e4m3fn, 7), "e5m2": (ml_dtypes.float8_e5m2, 14)}[fmt]
    v = np.moveaxis(np.asarray(x, np.float32).astype(ml_dtypes.bfloat16).astype(np.float64), axis, -1)
    blocks = v.reshape(v.shape[:-1] + (-1, 32))
    amax = np.abs(blocks).max(-1, keepdims=True)
    byte = np.maximum(np.where(amax > 0, np.frexp(amax)[1] - 1 + 127, 0) - down, 1)
    scale = np.exp2(byte - 127.0)
    codes = (blocks / scale).astype(np.float32).astype(dtype).astype(np.float64)
    return np.moveaxis((codes * scale).reshape(v.shape), -1, axis)


WIDE = False


def mx_kscale(k):
    if not WIDE:
        return np.ones(k)
    levels = np.array([10, -10, 5, -5, 0])
    if k % 512:
        return np.exp2(np.random.permutation(np.resize(levels, k // 32))).repeat(32)
    a = np.empty((k // 512, 16))
    for p in range(k // 512):
        a[p, :8] = np.random.permutation(np.resize(levels, 8))
        for g in range(8):
            far = levels[np.abs(levels - a[p, g]) >= 10]
            a[p, g + 8] = far[np.random.randint(len(far))]
    return np.exp2(a.ravel()).repeat(32)


def f64(x):
    return np.asarray(x).astype(np.float64)


def striped(idx):
    return np.tile(idx.reshape(-1, 16).T, (8, 1)).astype(np.uint16)


def unstriped(offs):
    return offs[:16].T.reshape(-1).astype(np.int64)


E2M1 = np.array([0.0, 0.5, 1.0, 1.5, 2.0, 3.0, 4.0, 6.0, -0.0, -0.5, -1.0, -1.5, -2.0, -3.0, -4.0, -6.0])


def pack_weight(w, fmt):
    k, n = w.shape
    w = f64(np.asarray(w, np.float32).astype(ml_dtypes.bfloat16)).reshape(k // 32, 32, n)
    amax = np.abs(w).max(1)
    if fmt == "e4m3":
        byte = np.frexp(amax)[1] - 1 + 127 - 7
    else:
        mant, ex = np.frexp(amax / 6.0)
        byte = np.where(mant > 0.5, ex, ex - 1) + 127
    byte = np.clip(np.where(amax > 0, byte, 1), 1, 254)
    scaled = (w * np.exp2(127.0 - byte)[:, None, :]).reshape(k, n).astype(np.float32)
    by_word = np.ascontiguousarray(scaled.reshape(k // 512, 128, 4, n).transpose(0, 1, 3, 2))
    if fmt == "e4m3":
        words = by_word.astype(ml_dtypes.float8_e4m3fn).view(np.uint8)
    else:
        c = by_word.astype(ml_dtypes.float4_e2m1fn).view(np.uint8) & 0xF
        words = (c[..., 0::2] | (c[..., 1::2] << 4)).reshape(k // 512, 128, 2 * n)
    return np.ascontiguousarray(words), np.ascontiguousarray(byte.astype(np.uint8).reshape(k // 512, 16, n))


def unpack_weight(words, scales, fmt):
    g, _, n = scales.shape
    words = np.ascontiguousarray(words).reshape(g, 128, n, -1)
    if fmt == "e4m3":
        vals = words.view(ml_dtypes.float8_e4m3fn).astype(np.float64)
    else:
        nib = np.empty((g, 128, n, 4), np.uint8)
        nib[..., 0::2] = words & 0xF
        nib[..., 1::2] = words >> 4
        vals = E2M1[nib]
    vals = vals * np.repeat(np.exp2(scales.astype(np.float64) - 127.0), 8, axis=1)[..., None]
    return vals.transpose(0, 1, 3, 2).reshape(g * 512, n)


def gelu(v):
    return 0.5 * v * (1.0 + np.tanh(np.sqrt(2.0 / np.pi) * (v + 0.044715 * v**3)))


K, M, H, T, S, T3, S2, P = 1536, 1024, 512, 4096, 1024, 2048, 512, 512

def setup_inputs():
    n = np.random.standard_normal
    s = mx_kscale(K)[:, None]
    u1 = mx_kscale(M)[:, None]
    u = mx_kscale(H)[:, None]
    d = {}
    d["tab_words"], d["tab_scales"] = pack_weight(n((K, T)) * s, "e4m3")
    d["offs"] = striped(np.random.permutation(T)[:S])
    d["tab2_words"], d["tab2_scales"] = pack_weight(n((H, T3)) / u / H ** 0.5, "e4m3")
    d["offs2"] = striped(np.random.permutation(T3)[:S2])
    d["pos1"] = striped(np.random.permutation(S)[:P])
    d["pos2"] = striped(np.random.permutation(S)[:P])
    d["w1"] = (1.5 * n((K, M)) / s / K ** 0.5).astype(np.float32)
    d["gain1"] = (np.exp(0.3 * n(M)) * u1[:, 0]).astype(np.float32)
    d["w2_words"], d["w2_scales"] = pack_weight(1.4 * n((M, H)) / u1 / M ** 0.5, "e2m1")
    d["gain2"] = (2.4 * np.exp(0.3 * n(H)) * u[:, 0]).astype(np.float32)
    d["cost"] = np.exp(0.4 * n(S2)).astype(np.float32)
    return d

def reference(tab_words, tab_scales, offs, tab2_words, tab2_scales, offs2, pos1, pos2, w1, gain1, w2_words, w2_scales, gain2, cost):
    v = unpack_weight(tab_words, tab_scales, "e4m3")[:, unstriped(offs)]
    v2 = unpack_weight(tab2_words, tab2_scales, "e4m3")[:, unstriped(offs2)]
    w2 = unpack_weight(w2_words, w2_scales, "e2m1")
    z1 = mxq(f64(w1), 0, "e4m3").T @ v
    a = z1 / (1.0 + np.exp(-z1)) * f64(gain1)[:, None]
    z2 = w2.T @ mxq(a, 0, "e4m3")
    h = np.tanh(z2) * f64(gain2)[:, None]
    e = v2.T @ mxq(h, 0, "e4m3")
    diff = e[:, unstriped(pos2)] - e[:, unstriped(pos1)]
    return f64(cost)[:, None] / (1.0 + np.exp(-diff))

@@ -1,0 +1,350 @@
+from contextlib import ExitStack
+
+import concourse.mybir as mybir
+
+K, M, H, T, S, T3, S2, PAIRS = 1536, 1024, 512, 4096, 1024, 2048, 512, 512
+FLOPS = 2 * (K * M * S + M * H * S + H * S2 * S)
+
+F32 = mybir.dt.float32
+BF16 = mybir.dt.bfloat16
+I32 = mybir.dt.int32
+U32 = mybir.dt.uint32
+U16 = mybir.dt.uint16
+U8 = mybir.dt.uint8
+FP8X4 = mybir.dt.float8_e4m3fn_x4
+FP4X4 = mybir.dt.float4_e2m1fn_x4
+ACT = mybir.ActivationFunctionType
+ALU = mybir.AluOpType
+
+P = 128
+PACK = 4
+KP = P * PACK
+CH = 128
+NCH = S // CH
+PASS1 = K // KP
+PASS2 = M // KP
+MT = S2 // P
+
+
+def tile_list_cushion_map_pairs_kernel(
+    tc, tab_words, tab_scales, offs, tab2_words, tab2_scales, offs2, pos1, pos2,
+    w1, gain1, w2_words, w2_scales, gain2, cost, out,
+):
+    nc = tc.nc
+    with ExitStack() as ctx:
+        keep = ctx.enter_context(tc.tile_pool(name="keep", bufs=1))
+        ring = ctx.enter_context(tc.tile_pool(name="ring", bufs=4))
+        psum = ctx.enter_context(tc.psum_pool(name="psum", bufs=1))
+
+        def kept(name, shape, dtype, tag=None):
+            return keep.tile(shape, dtype, name=name, tag=tag or name, align_bytes=64)
+
+        def bank(i):
+            return psum.tile([P, 512], F32, name="bank%d" % i)
+
+        offs_t = keep.tile([P, S // 16], U16, name="offs_t")
+        offs2_t = keep.tile([P, S2 // 16], U16, name="offs2_t")
+        pos1_t = keep.tile([P, PAIRS // 16], U16, name="pos1_t")
+        pos2_t = keep.tile([P, PAIRS // 16], U16, name="pos2_t")
+
+        tab_w = [kept("tab_w%d" % a, [P, T], I32) for a in range(PASS1)]
+        tab_s = kept("tab_s", [P, T], U8)
+        tab2_s = kept("tab2_s", [P, T3], U8)
+        w2_raw = kept("w2_raw", [P, PASS2, 2 * H], U8)
+        w2_sraw = kept("w2_sraw", [P, PASS2, H], U8)
+        w1_raw = {}
+        for b in range(PASS2):
+            for a in range(PASS1):
+                w1_raw[a, b] = kept("w1_raw%d_%d" % (a, b), [P, PACK, KP], F32)
+        g1 = kept("g1", [P, PASS2, PACK], F32)
+        g2 = kept("g2", [P, PACK], F32)
+        cost_t = kept("cost_t", [P, MT], F32)
+
+        zero_in = kept("zero_in", [P, 1], F32)
+        zero = kept("zero", [P, 1], F32)
+        nc.vector.memset(zero_in[:], 0.0)
+        nc.scalar.activation(zero[:], zero_in[:], ACT.Silu)
+        nc.vector.memset(tab_s[:].bitcast(I32), 0)
+        nc.vector.memset(w2_sraw[:].rearrange("p a c -> p (a c)").bitcast(I32), 0)
+        nc.vector.memset(tab2_s[:].bitcast(I32), 0)
+
+        def load_w1(a, b):
+            rows = w1[a * KP:(a + 1) * KP, b * KP:(b + 1) * KP]
+            nc.sync.dma_start(out=w1_raw[a, b][:], in_=rows.rearrange("(p j) c -> p j c", j=PACK))
+
+        def load_tab(a):
+            nc.sync.dma_start(out=tab_w[a][:], in_=tab_words[a].rearrange("p t i -> p (t i)").bitcast(I32))
+
+        load_tab(0)
+        nc.sync.dma_start(offs_t[:], offs)
+        for q in range(4):
+            nc.sync.dma_start(
+                out=tab_s[32 * q:32 * q + 4 * PASS1, :].bitcast(I32),
+                in_=tab_scales[:, 4 * q:4 * q + 4, :].bitcast(I32),
+            )
+        load_tab(1)
+        nc.sync.dma_start(out=w2_raw[:].bitcast(I32), in_=w2_words.rearrange("a p c -> p a c").bitcast(I32))
+        for q in range(4):
+            nc.sync.dma_start(
+                out=w2_sraw[32 * q:32 * q + 4, :, :].bitcast(I32),
+                in_=w2_scales[:, 4 * q:4 * q + 4, :].rearrange("a r c -> r a c").bitcast(I32),
+            )
+        load_tab(2)
+        nc.sync.dma_start(offs2_t[:], offs2)
+        for q in range(4):
+            nc.sync.dma_start(
+                out=tab2_s[32 * q:32 * q + 4, :].bitcast(I32),
+                in_=tab2_scales[0, 4 * q:4 * q + 4, :].bitcast(I32),
+            )
+        load_w1(0, 0)
+        load_w1(1, 0)
+        nc.sync.dma_start(out=g1[:], in_=gain1.rearrange("(b p t) -> p b t", b=PASS2, t=PACK))
+        load_w1(2, 0)
+        for a in range(PASS1):
+            load_w1(a, 1)
+        nc.sync.dma_start(out=g2[:], in_=gain2.rearrange("(p t) -> p t", t=PACK))
+        with nc.allow_non_contiguous_dma(reason="one cost value a partition"):
+            nc.sync.dma_start(out=cost_t[:], in_=cost.rearrange("(m p) -> p m", p=P))
+        nc.sync.dma_start(pos1_t[:], pos1)
+        nc.sync.dma_start(pos2_t[:], pos2)
+
+        w1_c, w1_s, w1_bf = {}, {}, {}
+
+        stage = [kept("stage%d" % c, [P, 2 * KP], F32) for c in range(NCH // 2)]
+
+        def round_w1(a, b, u, eng):
+            if b == 0:
+                bf = kept("w1_bf%d_%d" % (a, u), [P, 2 * KP], BF16, tag="tab_w%d" % (1 + u))[:]
+            else:
+                bf = stage[a][:, u * KP:(u + 1) * KP].bitcast(BF16)
+            w1_bf[a, b, u] = bf
+            dst = bf.rearrange("p (t m j) -> p m j t", t=2, j=PACK)
+            src = w1_raw[a, b][:].rearrange("p j (m t) -> p m j t", t=PACK)[:, :, :, 2 * u:2 * u + 2]
+            if eng == "s":
+                nc.scalar.copy(dst, src)
+            else:
+                nc.vector.tensor_copy(dst, src)
+
+        def quant_w1(a, b, u0, nu):
+            c = kept("w1_c%d_%d_%d" % (a, b, u0), [P, nu * 2 * P], U32)
+            s = kept("w1_s%d_%d_%d" % (a, b, u0), [P, nu * 2 * P], U8)
+            for t in range(2 * nu):
+                w1_c[a, b, 2 * u0 + t] = c[:, t * P:(t + 1) * P]
+                w1_s[a, b, 2 * u0 + t] = s[:, t * P:(t + 1) * P]
+            src = w1_bf[a, b, u0] if nu == 1 else stage[a][:].bitcast(BF16)
+            nc.vector.quantize_mx(out=c[:].bitcast(FP8X4), scales=s[:], in_=src)
+
+        v_w = [kept("v_w%d" % a, [P, S], U32) for a in range(PASS1)]
+
+        def gather_v(a):
+            nc.vector.tensor_copy(v_w[a][:], tab_w[a][:].bitcast(U32).indirect(offs_t[:]))
+
+        gather_v(0)
+        v_s = kept("v_s", [P, S], U8)
+        nc.vector.tensor_copy(v_s[:], tab_s[:].indirect(offs_t[:]))
+        gather_v(1)
+        w2_c = kept("w2_c", [P, PASS2, 2 * H], U8)
+        w2_s = kept("w2_s", [P, PASS2, H], U8)
+        nc.vector.tensor_copy(
+            w2_c[:].rearrange("p a (t m e) -> p a m t e", t=PACK, e=2),
+            w2_raw[:].rearrange("p a (m t e) -> p a m t e", t=PACK, e=2),
+        )
+        nc.vector.tensor_copy(
+            w2_s[:].rearrange("p a (t m) -> p a m t", t=PACK),
+            w2_sraw[:].rearrange("p a (m t) -> p a m t", t=PACK),
+        )
+        gather_v(2)
+        v2_s = kept("v2_s", [P, S2], U8)
+        nc.vector.tensor_copy(v2_s[:], tab2_s[:].indirect(offs2_t[:]))
+
+        z1 = {}
+
+        def mm1(a, b, c):
+            if a == 0:
+                z1[b, c] = bank(c)
+            cols = slice(c * CH, (c + 1) * CH)
+            for t in range(PACK):
+                nc.tensor.matmul_mx(
+                    out=z1[b, c][:, t * CH:(t + 1) * CH],
+                    lhsT=w1_c[a, b, t].bitcast(FP8X4),
+                    lhsT_scale=w1_s[a, b, t],
+                    rhs=v_w[a][:, cols].bitcast(FP8X4),
+                    rhs_scale=v_s[4 * a:P, cols],
+                    start=(a == 0 and t == 0),
+                    stop=(a == PASS1 - 1 and t == PACK - 1),
+                )
+
+        act_bf = {}
+
+        def staged(c, n):
+            return stage[c // 2][:, (c % 2) * KP:(c % 2 + n) * KP].rearrange("p (n t) -> p n t", t=PACK)
+
+        def activate(c, z, func):
+            nc.scalar.activation(staged(c, 1), z[:].rearrange("p (t n) -> p n t", t=PACK), func, bias=zero[:])
+
+        def apply_gain(key, c, n, gain_cols):
+            bf = ring.tile([P, n * KP], BF16, name="act_bf", align_bytes=64)
+            act_bf[key, c] = bf
+            nc.vector.tensor_tensor(
+                bf[:].rearrange("p (n t) -> p n t", t=PACK),
+                staged(c, n),
+                gain_cols.unsqueeze(1).to_broadcast([P, n * CH, PACK]),
+                ALU.mult,
+            )
+
+        a_c = [kept("a_c%d" % b, [P, S], U32) for b in range(PASS2)]
+        a_s = [kept("a_s%d" % b, [P, S], U8) for b in range(PASS2)]
+        h_c = kept("h_c", [P, S], U32)
+        h_s = kept("h_s", [P, S], U8)
+
+        def quant(key, codes, scales, c, n):
+            cols = slice(c * CH, (c + n) * CH)
+            nc.vector.quantize_mx(out=codes[:, cols].bitcast(FP8X4), scales=scales[:, cols], in_=act_bf[key, c][:])
+
+        def silu(b, c):
+            activate(c, z1[b, c], ACT.Silu)
+
+        def gain_a(b, c, n):
+            apply_gain(b, c, n, g1[:, b, :])
+
+        def quant_a(b, c, n):
+            quant(b, a_c[b], a_s[b], c, n)
+
+        def tanh(c):
+            activate(c, z2[c], ACT.Tanh)
+
+        def gain_h(c, n):
+            apply_gain("h", c, n, g2[:, :])
+
+        def quant_h(c, n):
+            quant("h", h_c, h_s, c, n)
+
+        z2 = {}
+
+        def mm2(c):
+            z2[c] = bank(c)
+            cols = slice(c * CH, (c + 1) * CH)
+            for b in range(PASS2):
+                for t in range(PACK):
+                    nc.tensor.matmul_mx(
+                        out=z2[c][:, t * CH:(t + 1) * CH],
+                        lhsT=w2_c[:, b, 2 * t * P:2 * (t + 1) * P].bitcast(FP4X4),
+                        lhsT_scale=w2_s[:, b, t * P:(t + 1) * P],
+                        rhs=a_c[b][:, cols].bitcast(FP8X4),
+                        rhs_scale=a_s[b][:, cols],
+                        start=(b == 0 and t == 0),
+                        stop=(b == PASS2 - 1 and t == PACK - 1),
+                    )
+
+        for a in range(PASS1):
+            round_w1(a, 0, 0, "s")
+            round_w1(a, 0, 1, "v")
+            quant_w1(a, 0, 1, 1)
+            quant_w1(a, 0, 0, 1)
+            for c in range(NCH):
+                mm1(a, 0, c)
+
+        for a in range(PASS1):
+            c = 2 * a
+            silu(0, c)
+            if a == 0:
+                gain_a(0, c, 1)
+            silu(0, c + 1)
+            if a == 0:
+                gain_a(0, c + 1, 1)
+                quant_a(0, c, 1)
+            else:
+                gain_a(0, c, 2)
+            round_w1(a, 1, 0, "s")
+            round_w1(a, 1, 1, "v")
+            if a == 0:
+                quant_a(0, c + 1, 1)
+            else:
+                quant_a(0, c, 2)
+            quant_w1(a, 1, 0, 2)
+        silu(0, 6)
+        silu(0, 7)
+        gain_a(0, 6, 2)
+        quant_a(0, 6, 2)
+
+        tab2_w = kept("tab2_w", [P, T3], I32, tag="w1_raw2_1")
+        nc.sync.dma_start(out=tab2_w[:], in_=tab2_words[0].rearrange("p t i -> p (t i)").bitcast(I32))
+        v2_w = kept("v2_w", [P, S2], U32)
+        e = [kept("e%d" % m, [P, S], F32) for m in range(MT)]
+
+        def mm3(m, dst, lo, hi):
+            rows = slice(m * P, (m + 1) * P)
+            nc.tensor.matmul_mx(
+                out=dst, lhsT=v2_w[:, rows].bitcast(FP8X4), lhsT_scale=v2_s[:, rows],
+                rhs=h_c[:, lo:hi].bitcast(FP8X4), rhs_scale=h_s[:, lo:hi], start=True, stop=True,
+            )
+
+        eb = {}
+        for c in range(0, NCH, 2):
+            for i in (c, c + 1):
+                for a in range(PASS1):
+                    mm1(a, 1, i)
+                silu(1, i)
+            gain_a(1, c, 2)
+            if c >= 4:
+                quant_h(c - 4, 2)
+            if c >= 2:
+                tanh(c - 2)
+                tanh(c - 1)
+            quant_a(1, c, 2)
+            mm2(c)
+            mm2(c + 1)
+            if c >= 2:
+                gain_h(c - 2, 2)
+            if c == 2:
+                nc.vector.tensor_copy(v2_w[:], tab2_w[:].bitcast(U32).indirect(offs2_t[:]))
+        for m in range(MT):
+            eb[m, 0] = bank(m)
+            mm3(m, eb[m, 0][:], 0, 512)
+        tanh(6)
+        quant_h(4, 2)
+        gain_h(6, 1)
+        tanh(7)
+        nc.scalar.copy(e[0][:, 0:512], eb[0, 0][:])
+        gain_h(7, 1)
+        quant_h(6, 1)
+        quant_h(7, 1)
+        eb[0, 1] = bank(4)
+        mm3(0, eb[0, 1][:, 0:256], 512, 768)
+        mm3(0, eb[0, 1][:, 256:384], 768, 896)
+        nc.scalar.copy(e[0][:, 512:896], eb[0, 1][:, 0:384])
+        eb[0, 2] = bank(5)
+        mm3(0, eb[0, 2][:, 0:128], 896, 1024)
+        nc.vector.tensor_copy(e[0][:, 896:1024], eb[0, 2][:, 0:128])
+        for m, bk in ((1, 6), (2, 7), (3, 0)):
+            eb[m, 1] = bank(bk)
+            mm3(m, eb[m, 1][:], 512, 1024)
+
+        half_cost = kept("half_cost", [P, MT], F32, tag="w1_raw1_1")
+        nc.vector.tensor_scalar(half_cost[:], cost_t[:], 0.5, None, ALU.mult)
+
+        def finish(m, lo, hi, last):
+            n = hi - lo
+            before = ring.tile([P, n], F32, name="before", align_bytes=64)
+            diff = ring.tile([P, n], F32, name="diff", align_bytes=64)
+            th = ring.tile([P, n], F32, name="th", align_bytes=64)
+            res = ring.tile([P, n], F32, name="res", align_bytes=64)
+            nc.vector.tensor_copy(before[:], e[m][:].indirect(pos1_t[:, lo // 16:hi // 16]))
+            nc.vector.tensor_tensor(diff[:], e[m][:].indirect(pos2_t[:, lo // 16:hi // 16]), before[:], ALU.subtract)
+            nc.scalar.activation(th[:], diff[:], ACT.Tanh, bias=zero[:], scale=0.5)
+            hc = half_cost[:, m:m + 1]
+            if last:
+                nc.vector.tensor_scalar(res[:], th[:], hc, hc, ALU.mult, ALU.add)
+            else:
+                nc.scalar.activation(res[:], th[:], ACT.Identity, bias=hc, scale=hc)
+            nc.sync.dma_start(out=out[m * P:(m + 1) * P, lo:hi], in_=res[:])
+
+        for m in range(MT):
+            if m + 1 < MT:
+                nc.scalar.copy(e[m + 1][:, 0:512], eb[m + 1, 0][:])
+                nc.scalar.copy(e[m + 1][:, 512:1024], eb[m + 1, 1][:])
+            if m + 1 < MT:
+                finish(m, 0, PAIRS, False)
+            else:
+                finish(m, 0, 384, False)
+                finish(m, 384, PAIRS, True)

@@ -62,11 +62,11 @@ def tile_list_cushion_map_pairs_kernel(
 
         zero_in = kept("zero_in", [P, 1], F32)
         zero = kept("zero", [P, 1], F32)
+        nc.vector.memset(tab_s[:].bitcast(I32), 0)
+        nc.gpsimd.memset(w2_sraw[:].rearrange("p a c -> p (a c)").bitcast(I32), 0)
+        nc.gpsimd.memset(tab2_s[:].bitcast(I32), 0)
         nc.vector.memset(zero_in[:], 0.0)
         nc.scalar.activation(zero[:], zero_in[:], ACT.Silu)
-        nc.vector.memset(tab_s[:].bitcast(I32), 0)
-        nc.vector.memset(w2_sraw[:].rearrange("p a c -> p (a c)").bitcast(I32), 0)
-        nc.vector.memset(tab2_s[:].bitcast(I32), 0)
 
         def load_w1(a, b):
             rows = w1[a * KP:(a + 1) * KP, b * KP:(b + 1) * KP]
@@ -98,8 +98,8 @@ def tile_list_cushion_map_pairs_kernel(
             )
         load_w1(0, 0)
         load_w1(1, 0)
-        nc.sync.dma_start(out=g1[:], in_=gain1.rearrange("(b p t) -> p b t", b=PASS2, t=PACK))
         load_w1(2, 0)
+        nc.sync.dma_start(out=g1[:], in_=gain1.rearrange("(b p t) -> p b t", b=PASS2, t=PACK))
         for a in range(PASS1):
             load_w1(a, 1)
         nc.sync.dma_start(out=g2[:], in_=gain2.rearrange("(p t) -> p t", t=PACK))
@@ -108,31 +108,25 @@ def tile_list_cushion_map_pairs_kernel(
         nc.sync.dma_start(pos1_t[:], pos1)
         nc.sync.dma_start(pos2_t[:], pos2)
 
-        w1_c, w1_s, w1_bf = {}, {}, {}
+        w1_c, w1_s = {}, {}
 
         stage = [kept("stage%d" % c, [P, 2 * KP], F32) for c in range(NCH // 2)]
 
-        def round_w1(a, b, u, eng):
-            if b == 0:
-                bf = kept("w1_bf%d_%d" % (a, u), [P, 2 * KP], BF16, tag="tab_w%d" % (1 + u))[:]
-            else:
-                bf = stage[a][:, u * KP:(u + 1) * KP].bitcast(BF16)
-            w1_bf[a, b, u] = bf
-            dst = bf.rearrange("p (t m j) -> p m j t", t=2, j=PACK)
-            src = w1_raw[a, b][:].rearrange("p j (m t) -> p m j t", t=PACK)[:, :, :, 2 * u:2 * u + 2]
+        def round_w1(a, b, u0, nu, eng, bf):
+            dst = bf.rearrange("p (t m j) -> p m j t", t=2 * nu, j=PACK)
+            src = w1_raw[a, b][:].rearrange("p j (m t) -> p m j t", t=PACK)[:, :, :, 2 * u0:2 * (u0 + nu)]
             if eng == "s":
                 nc.scalar.copy(dst, src)
             else:
                 nc.vector.tensor_copy(dst, src)
 
-        def quant_w1(a, b, u0, nu):
+        def quant_w1(a, b, u0, nu, bf):
             c = kept("w1_c%d_%d_%d" % (a, b, u0), [P, nu * 2 * P], U32)
             s = kept("w1_s%d_%d_%d" % (a, b, u0), [P, nu * 2 * P], U8)
             for t in range(2 * nu):
                 w1_c[a, b, 2 * u0 + t] = c[:, t * P:(t + 1) * P]
                 w1_s[a, b, 2 * u0 + t] = s[:, t * P:(t + 1) * P]
-            src = w1_bf[a, b, u0] if nu == 1 else stage[a][:].bitcast(BF16)
-            nc.vector.quantize_mx(out=c[:].bitcast(FP8X4), scales=s[:], in_=src)
+            nc.vector.quantize_mx(out=c[:].bitcast(FP8X4), scales=s[:], in_=bf)
 
         v_w = [kept("v_w%d" % a, [P, S], U32) for a in range(PASS1)]
 
@@ -146,12 +140,12 @@ def tile_list_cushion_map_pairs_kernel(
         w2_c = kept("w2_c", [P, PASS2, 2 * H], U8)
         w2_s = kept("w2_s", [P, PASS2, H], U8)
         nc.vector.tensor_copy(
-            w2_c[:].rearrange("p a (t m e) -> p a m t e", t=PACK, e=2),
-            w2_raw[:].rearrange("p a (m t e) -> p a m t e", t=PACK, e=2),
+            w2_c[:].rearrange("p a (t m e) -> p a t m e", t=PACK, e=2),
+            w2_raw[:].rearrange("p a (m t e) -> p a t m e", t=PACK, e=2),
         )
         nc.vector.tensor_copy(
-            w2_s[:].rearrange("p a (t m) -> p a m t", t=PACK),
-            w2_sraw[:].rearrange("p a (m t) -> p a m t", t=PACK),
+            w2_s[:].rearrange("p a (t m) -> p a t m", t=PACK),
+            w2_sraw[:].rearrange("p a (m t) -> p a t m", t=PACK),
         )
         gather_v(2)
         v2_s = kept("v2_s", [P, S2], U8)
@@ -237,35 +231,40 @@ def tile_list_cushion_map_pairs_kernel(
                     )
 
         for a in range(PASS1):
-            round_w1(a, 0, 0, "s")
-            round_w1(a, 0, 1, "v")
-            quant_w1(a, 0, 1, 1)
-            quant_w1(a, 0, 0, 1)
+            bf = [kept("w1_bf%d_%d" % (a, u), [P, 2 * KP], BF16, tag="tab_w%d" % (1 + u))[:] for u in range(2)]
+            round_w1(a, 0, 0, 1, "s", bf[0])
+            round_w1(a, 0, 1, 1, "v", bf[1])
+            quant_w1(a, 0, 1, 1, bf[1])
+            quant_w1(a, 0, 0, 1, bf[0])
             for c in range(NCH):
                 mm1(a, 0, c)
 
-        for a in range(PASS1):
-            c = 2 * a
+        def round_shared(a, holder):
+            round_w1(a, 1, 0, 1, "s", holder[:, 0:KP].bitcast(BF16))
+            round_w1(a, 1, 1, 1, "v", holder[:, KP:2 * KP].bitcast(BF16))
+
+        bf01 = kept("w1_bf01", [P, 4 * KP], BF16, tag="tab_w1")
+        round_w1(0, 1, 0, 2, "v", bf01[:])
+        silu(0, 0)
+        gain_a(0, 0, 1)
+        silu(0, 1)
+        quant_w1(0, 1, 0, 2, bf01[:])
+        gain_a(0, 1, 1)
+        quant_a(0, 0, 1)
+        round_shared(1, stage[0])
+        quant_a(0, 1, 1)
+        silu(0, 2)
+        silu(0, 3)
+        gain_a(0, 2, 2)
+        quant_w1(1, 1, 0, 2, stage[0][:].bitcast(BF16))
+        round_shared(2, stage[1])
+        quant_a(0, 2, 2)
+        quant_w1(2, 1, 0, 2, stage[1][:].bitcast(BF16))
+        for c in (4, 6):
             silu(0, c)
-            if a == 0:
-                gain_a(0, c, 1)
             silu(0, c + 1)
-            if a == 0:
-                gain_a(0, c + 1, 1)
-                quant_a(0, c, 1)
-            else:
-                gain_a(0, c, 2)
-            round_w1(a, 1, 0, "s")
-            round_w1(a, 1, 1, "v")
-            if a == 0:
-                quant_a(0, c + 1, 1)
-            else:
-                quant_a(0, c, 2)
-            quant_w1(a, 1, 0, 2)
-        silu(0, 6)
-        silu(0, 7)
-        gain_a(0, 6, 2)
-        quant_a(0, 6, 2)
+            gain_a(0, c, 2)
+            quant_a(0, c, 2)
 
         tab2_w = kept("tab2_w", [P, T3], I32, tag="w1_raw2_1")
         nc.sync.dma_start(out=tab2_w[:], in_=tab2_words[0].rearrange("p t i -> p (t i)").bitcast(I32))
@@ -280,7 +279,7 @@ def tile_list_cushion_map_pairs_kernel(
             )
 
         eb = {}
-        for c in range(0, NCH, 2):
+        for c in range(0, NCH - 2, 2):
             for i in (c, c + 1):
                 for a in range(PASS1):
                     mm1(a, 1, i)
@@ -298,13 +297,27 @@ def tile_list_cushion_map_pairs_kernel(
                 gain_h(c - 2, 2)
             if c == 2:
                 nc.vector.tensor_copy(v2_w[:], tab2_w[:].bitcast(U32).indirect(offs2_t[:]))
+        for i in (6, 7):
+            for a in range(PASS1):
+                mm1(a, 1, i)
+            silu(1, i)
+            gain_a(1, i, 1)
+            if i == 6:
+                quant_h(2, 2)
+        quant_a(1, 6, 1)
+        mm2(6)
+        tanh(4)
+        tanh(5)
+        quant_a(1, 7, 1)
+        mm2(7)
+        gain_h(4, 2)
         for m in range(MT):
             eb[m, 0] = bank(m)
             mm3(m, eb[m, 0][:], 0, 512)
         tanh(6)
-        quant_h(4, 2)
-        gain_h(6, 1)
         tanh(7)
+        gain_h(6, 1)
+        quant_h(4, 2)
         nc.scalar.copy(e[0][:, 0:512], eb[0, 0][:])
         gain_h(7, 1)
         quant_h(6, 1)
@@ -346,5 +359,5 @@ def tile_list_cushion_map_pairs_kernel(
             if m + 1 < MT:
                 finish(m, 0, PAIRS, False)
             else:
-                finish(m, 0, 384, False)
+                finish(m, 0, 384, True)
                 finish(m, 384, PAIRS, True)

@@ -82,22 +82,22 @@ def tile_list_cushion_map_pairs_kernel(
                 out=tab_s[32 * q:32 * q + 4 * PASS1, :].bitcast(I32),
                 in_=tab_scales[:, 4 * q:4 * q + 4, :].bitcast(I32),
             )
-        load_tab(1)
+        load_w1(0, 0)
         nc.sync.dma_start(out=w2_raw[:].bitcast(I32), in_=w2_words.rearrange("a p c -> p a c").bitcast(I32))
         for q in range(4):
             nc.sync.dma_start(
                 out=w2_sraw[32 * q:32 * q + 4, :, :].bitcast(I32),
                 in_=w2_scales[:, 4 * q:4 * q + 4, :].rearrange("a r c -> r a c").bitcast(I32),
             )
-        load_tab(2)
+        load_tab(1)
         nc.sync.dma_start(offs2_t[:], offs2)
         for q in range(4):
             nc.sync.dma_start(
                 out=tab2_s[32 * q:32 * q + 4, :].bitcast(I32),
                 in_=tab2_scales[0, 4 * q:4 * q + 4, :].bitcast(I32),
             )
-        load_w1(0, 0)
         load_w1(1, 0)
+        load_tab(2)
         load_w1(2, 0)
         nc.sync.dma_start(out=g1[:], in_=gain1.rearrange("(b p t) -> p b t", b=PASS2, t=PACK))
         for a in range(PASS1):
@@ -128,15 +128,15 @@ def tile_list_cushion_map_pairs_kernel(
                 w1_s[a, b, 2 * u0 + t] = s[:, t * P:(t + 1) * P]
             nc.vector.quantize_mx(out=c[:].bitcast(FP8X4), scales=s[:], in_=bf)
 
-        v_w = [kept("v_w%d" % a, [P, S], U32) for a in range(PASS1)]
+        v_w = {}
 
         def gather_v(a):
+            v_w[a] = kept("v_w%d" % a, [P, S], U32, tag=("tab_w%d" % (a - 1) if a else None))
             nc.vector.tensor_copy(v_w[a][:], tab_w[a][:].bitcast(U32).indirect(offs_t[:]))
 
         gather_v(0)
         v_s = kept("v_s", [P, S], U8)
         nc.vector.tensor_copy(v_s[:], tab_s[:].indirect(offs_t[:]))
-        gather_v(1)
         w2_c = kept("w2_c", [P, PASS2, 2 * H], U8)
         w2_s = kept("w2_s", [P, PASS2, H], U8)
         nc.vector.tensor_copy(
@@ -147,7 +147,6 @@ def tile_list_cushion_map_pairs_kernel(
             w2_s[:].rearrange("p a (t m) -> p a t m", t=PACK),
             w2_sraw[:].rearrange("p a (m t) -> p a t m", t=PACK),
         )
-        gather_v(2)
         v2_s = kept("v2_s", [P, S2], U8)
         nc.vector.tensor_copy(v2_s[:], tab2_s[:].indirect(offs2_t[:]))
 
@@ -231,11 +230,17 @@ def tile_list_cushion_map_pairs_kernel(
                     )
 
         for a in range(PASS1):
-            bf = [kept("w1_bf%d_%d" % (a, u), [P, 2 * KP], BF16, tag="tab_w%d" % (1 + u))[:] for u in range(2)]
-            round_w1(a, 0, 0, 1, "s", bf[0])
-            round_w1(a, 0, 1, 1, "v", bf[1])
-            quant_w1(a, 0, 1, 1, bf[1])
-            quant_w1(a, 0, 0, 1, bf[0])
+            if a:
+                gather_v(a)
+            bf = kept("w1_bf%d" % a, [P, 4 * KP], BF16, tag="tab_w%d" % a)
+            if a < PASS1 - 1:
+                round_w1(a, 0, 0, 2, "s", bf[:])
+                quant_w1(a, 0, 0, 2, bf[:])
+            else:
+                round_w1(a, 0, 0, 1, "s", bf[:, 0:2 * KP])
+                round_w1(a, 0, 1, 1, "v", bf[:, 2 * KP:4 * KP])
+                quant_w1(a, 0, 1, 1, bf[:, 2 * KP:4 * KP])
+                quant_w1(a, 0, 0, 1, bf[:, 0:2 * KP])
             for c in range(NCH):
                 mm1(a, 0, c)
 
@@ -243,7 +248,7 @@ def tile_list_cushion_map_pairs_kernel(
             round_w1(a, 1, 0, 1, "s", holder[:, 0:KP].bitcast(BF16))
             round_w1(a, 1, 1, 1, "v", holder[:, KP:2 * KP].bitcast(BF16))
 
-        bf01 = kept("w1_bf01", [P, 4 * KP], BF16, tag="tab_w1")
+        bf01 = kept("w1_bf01", [P, 4 * KP], BF16, tag="tab_w2")
         round_w1(0, 1, 0, 2, "v", bf01[:])
         silu(0, 0)
         gain_a(0, 0, 1)
@@ -264,7 +269,7 @@ def tile_list_cushion_map_pairs_kernel(
             silu(0, c)
             silu(0, c + 1)
             gain_a(0, c, 2)
-            quant_a(0, c, 2)
+        quant_a(0, 4, 2)
 
         tab2_w = kept("tab2_w", [P, T3], I32, tag="w1_raw2_1")
         nc.sync.dma_start(out=tab2_w[:], in_=tab2_words[0].rearrange("p t i -> p (t i)").bitcast(I32))
@@ -285,6 +290,10 @@ def tile_list_cushion_map_pairs_kernel(
                     mm1(a, 1, i)
                 silu(1, i)
             gain_a(1, c, 2)
+            if c == 0:
+                quant_a(0, 6, 2)
+            if c == 2:
+                nc.vector.tensor_copy(v2_w[:], tab2_w[:].bitcast(U32).indirect(offs2_t[:]))
             if c >= 4:
                 quant_h(c - 4, 2)
             if c >= 2:
@@ -295,8 +304,6 @@ def tile_list_cushion_map_pairs_kernel(
             mm2(c + 1)
             if c >= 2:
                 gain_h(c - 2, 2)
-            if c == 2:
-                nc.vector.tensor_copy(v2_w[:], tab2_w[:].bitcast(U32).indirect(offs2_t[:]))
         for i in (6, 7):
             for a in range(PASS1):
                 mm1(a, 1, i)
@@ -336,14 +343,20 @@ def tile_list_cushion_map_pairs_kernel(
         half_cost = kept("half_cost", [P, MT], F32, tag="w1_raw1_1")
         nc.vector.tensor_scalar(half_cost[:], cost_t[:], 0.5, None, ALU.mult)
 
+        before = {}
+
+        def pick_before(m):
+            before[m] = ring.tile([P, PAIRS], F32, name="before", align_bytes=64)
+            nc.vector.tensor_copy(before[m][:], e[m][:].indirect(pos1_t[:]))
+
         def finish(m, lo, hi, last):
             n = hi - lo
-            before = ring.tile([P, n], F32, name="before", align_bytes=64)
             diff = ring.tile([P, n], F32, name="diff", align_bytes=64)
             th = ring.tile([P, n], F32, name="th", align_bytes=64)
             res = ring.tile([P, n], F32, name="res", align_bytes=64)
-            nc.vector.tensor_copy(before[:], e[m][:].indirect(pos1_t[:, lo // 16:hi // 16]))
-            nc.vector.tensor_tensor(diff[:], e[m][:].indirect(pos2_t[:, lo // 16:hi // 16]), before[:], ALU.subtract)
+            nc.vector.tensor_tensor(
+                diff[:], e[m][:].indirect(pos2_t[:, lo // 16:hi // 16]), before[m][:, lo:hi], ALU.subtract
+            )
             nc.scalar.activation(th[:], diff[:], ACT.Tanh, bias=zero[:], scale=0.5)
             hc = half_cost[:, m:m + 1]
             if last:
@@ -352,11 +365,12 @@ def tile_list_cushion_map_pairs_kernel(
                 nc.scalar.activation(res[:], th[:], ACT.Identity, bias=hc, scale=hc)
             nc.sync.dma_start(out=out[m * P:(m + 1) * P, lo:hi], in_=res[:])
 
+        pick_before(0)
         for m in range(MT):
             if m + 1 < MT:
                 nc.scalar.copy(e[m + 1][:, 0:512], eb[m + 1, 0][:])
                 nc.scalar.copy(e[m + 1][:, 512:1024], eb[m + 1, 1][:])
-            if m + 1 < MT:
+                pick_before(m + 1)
                 finish(m, 0, PAIRS, False)
             else:
                 finish(m, 0, 384, True)

@@ -55,16 +55,18 @@ def tile_list_cushion_map_pairs_kernel(
         w1_raw = {}
         for b in range(PASS2):
             for a in range(PASS1):
-                w1_raw[a, b] = kept("w1_raw%d_%d" % (a, b), [P, PACK, KP], F32)
+                if (a, b) != (0, 1):
+                    w1_raw[a, b] = kept("w1_raw%d_%d" % (a, b), [P, PACK, KP], F32)
+        w1_half = [kept("w1_half%d" % half, [P, PACK, KP // 2], F32) for half in range(2)]
         g1 = kept("g1", [P, PASS2, PACK], F32)
         g2 = kept("g2", [P, PACK], F32)
         cost_t = kept("cost_t", [P, MT], F32)
 
         zero_in = kept("zero_in", [P, 1], F32)
         zero = kept("zero", [P, 1], F32)
-        nc.vector.memset(tab_s[:].bitcast(I32), 0)
-        nc.gpsimd.memset(w2_sraw[:].rearrange("p a c -> p (a c)").bitcast(I32), 0)
-        nc.gpsimd.memset(tab2_s[:].bitcast(I32), 0)
+        nc.gpsimd.memset(tab_s[:].bitcast(I32), 0)
+        nc.vector.memset(w2_sraw[:].rearrange("p a c -> p (a c)").bitcast(I32), 0)
+        nc.vector.memset(tab2_s[:].bitcast(I32), 0)
         nc.vector.memset(zero_in[:], 0.0)
         nc.scalar.activation(zero[:], zero_in[:], ACT.Silu)
 
@@ -78,7 +80,7 @@ def tile_list_cushion_map_pairs_kernel(
         load_tab(0)
         nc.sync.dma_start(offs_t[:], offs)
         for q in range(4):
-            nc.sync.dma_start(
+            nc.gpsimd.dma_start(
                 out=tab_s[32 * q:32 * q + 4 * PASS1, :].bitcast(I32),
                 in_=tab_scales[:, 4 * q:4 * q + 4, :].bitcast(I32),
             )
@@ -99,8 +101,11 @@ def tile_list_cushion_map_pairs_kernel(
         load_w1(1, 0)
         load_tab(2)
         load_w1(2, 0)
+        for half in range(2):
+            rows = w1[0:KP, KP + half * KP // 2:KP + (half + 1) * KP // 2]
+            nc.sync.dma_start(out=w1_half[half][:], in_=rows.rearrange("(p j) c -> p j c", j=PACK))
         nc.sync.dma_start(out=g1[:], in_=gain1.rearrange("(b p t) -> p b t", b=PASS2, t=PACK))
-        for a in range(PASS1):
+        for a in range(1, PASS1):
             load_w1(a, 1)
         nc.sync.dma_start(out=g2[:], in_=gain2.rearrange("(p t) -> p t", t=PACK))
         with nc.allow_non_contiguous_dma(reason="one cost value a partition"):
@@ -135,8 +140,6 @@ def tile_list_cushion_map_pairs_kernel(
             nc.vector.tensor_copy(v_w[a][:], tab_w[a][:].bitcast(U32).indirect(offs_t[:]))
 
         gather_v(0)
-        v_s = kept("v_s", [P, S], U8)
-        nc.vector.tensor_copy(v_s[:], tab_s[:].indirect(offs_t[:]))
         w2_c = kept("w2_c", [P, PASS2, 2 * H], U8)
         w2_s = kept("w2_s", [P, PASS2, H], U8)
         nc.vector.tensor_copy(
@@ -147,6 +150,8 @@ def tile_list_cushion_map_pairs_kernel(
             w2_s[:].rearrange("p a (t m) -> p a t m", t=PACK),
             w2_sraw[:].rearrange("p a (m t) -> p a t m", t=PACK),
         )
+        v_s = kept("v_s", [P, S], U8)
+        nc.vector.tensor_copy(v_s[:], tab_s[:].indirect(offs_t[:]))
         v2_s = kept("v2_s", [P, S2], U8)
         nc.vector.tensor_copy(v2_s[:], tab2_s[:].indirect(offs2_t[:]))
 
@@ -249,7 +254,11 @@ def tile_list_cushion_map_pairs_kernel(
             round_w1(a, 1, 1, 1, "v", holder[:, KP:2 * KP].bitcast(BF16))
 
         bf01 = kept("w1_bf01", [P, 4 * KP], BF16, tag="tab_w2")
-        round_w1(0, 1, 0, 2, "v", bf01[:])
+        for half in range(2):
+            nc.vector.tensor_copy(
+                bf01[:].rearrange("p (t m j) -> p m j t", t=PACK, j=PACK)[:, half * P // 2:(half + 1) * P // 2],
+                w1_half[half][:].rearrange("p j (m t) -> p m j t", t=PACK),
+            )
         silu(0, 0)
         gain_a(0, 0, 1)
         silu(0, 1)

from contextlib import ExitStack

import concourse.mybir as mybir

K, M, H, T, S, T3, S2, PAIRS = 1536, 1024, 512, 4096, 1024, 2048, 512, 512
FLOPS = 2 * (K * M * S + M * H * S + H * S2 * S)

F32 = mybir.dt.float32
BF16 = mybir.dt.bfloat16
I32 = mybir.dt.int32
U32 = mybir.dt.uint32
U16 = mybir.dt.uint16
U8 = mybir.dt.uint8
FP8X4 = mybir.dt.float8_e4m3fn_x4
FP4X4 = mybir.dt.float4_e2m1fn_x4
ACT = mybir.ActivationFunctionType
ALU = mybir.AluOpType

P = 128
PACK = 4
KP = P * PACK
CH = 128
NCH = S // CH
PASS1 = K // KP
PASS2 = M // KP
MT = S2 // P


def tile_list_cushion_map_pairs_kernel(
    tc, tab_words, tab_scales, offs, tab2_words, tab2_scales, offs2, pos1, pos2,
    w1, gain1, w2_words, w2_scales, gain2, cost, out,
):
    nc = tc.nc
    with ExitStack() as ctx:
        keep = ctx.enter_context(tc.tile_pool(name="keep", bufs=1))
        ring = ctx.enter_context(tc.tile_pool(name="ring", bufs=4))
        psum = ctx.enter_context(tc.psum_pool(name="psum", bufs=1))

        def kept(name, shape, dtype, tag=None):
            return keep.tile(shape, dtype, name=name, tag=tag or name, align_bytes=64)

        def bank(i):
            return psum.tile([P, 512], F32, name="bank%d" % i)

        offs_t = keep.tile([P, S // 16], U16, name="offs_t")
        offs2_t = keep.tile([P, S2 // 16], U16, name="offs2_t")
        pos1_t = keep.tile([P, PAIRS // 16], U16, name="pos1_t")
        pos2_t = keep.tile([P, PAIRS // 16], U16, name="pos2_t")

        tab_w = [kept("tab_w%d" % a, [P, T], I32) for a in range(PASS1)]
        tab_s = kept("tab_s", [P, T], U8)
        tab2_s = kept("tab2_s", [P, T3], U8)
        w2_raw = kept("w2_raw", [P, PASS2, 2 * H], U8)
        w2_sraw = kept("w2_sraw", [P, PASS2, H], U8)
        w1_raw = {}
        for b in range(PASS2):
            for a in range(PASS1):
                if (a, b) != (0, 1):
                    w1_raw[a, b] = kept("w1_raw%d_%d" % (a, b), [P, PACK, KP], F32)
        w1_half = [kept("w1_half%d" % half, [P, PACK, KP // 2], F32) for half in range(2)]
        g1 = kept("g1", [P, PASS2, PACK], F32)
        g2 = kept("g2", [P, PACK], F32)
        cost_t = kept("cost_t", [P, MT], F32)

        zero_in = kept("zero_in", [P, 1], F32)
        zero = kept("zero", [P, 1], F32)
        nc.gpsimd.memset(tab_s[:].bitcast(I32), 0)
        nc.vector.memset(w2_sraw[:].rearrange("p a c -> p (a c)").bitcast(I32), 0)
        nc.vector.memset(tab2_s[:].bitcast(I32), 0)
        nc.vector.memset(zero_in[:], 0.0)
        nc.scalar.activation(zero[:], zero_in[:], ACT.Silu)

        def load_w1(a, b):
            rows = w1[a * KP:(a + 1) * KP, b * KP:(b + 1) * KP]
            nc.sync.dma_start(out=w1_raw[a, b][:], in_=rows.rearrange("(p j) c -> p j c", j=PACK))

        def load_tab(a):
            nc.sync.dma_start(out=tab_w[a][:], in_=tab_words[a].rearrange("p t i -> p (t i)").bitcast(I32))

        load_tab(0)
        nc.sync.dma_start(offs_t[:], offs)
        for q in range(4):
            nc.gpsimd.dma_start(
                out=tab_s[32 * q:32 * q + 4 * PASS1, :].bitcast(I32),
                in_=tab_scales[:, 4 * q:4 * q + 4, :].bitcast(I32),
            )
        load_w1(0, 0)
        nc.sync.dma_start(out=w2_raw[:].bitcast(I32), in_=w2_words.rearrange("a p c -> p a c").bitcast(I32))
        for q in range(4):
            nc.sync.dma_start(
                out=w2_sraw[32 * q:32 * q + 4, :, :].bitcast(I32),
                in_=w2_scales[:, 4 * q:4 * q + 4, :].rearrange("a r c -> r a c").bitcast(I32),
            )
        load_tab(1)
        nc.sync.dma_start(offs2_t[:], offs2)
        for q in range(4):
            nc.sync.dma_start(
                out=tab2_s[32 * q:32 * q + 4, :].bitcast(I32),
                in_=tab2_scales[0, 4 * q:4 * q + 4, :].bitcast(I32),
            )
        load_w1(1, 0)
        load_tab(2)
        load_w1(2, 0)
        for half in range(2):
            rows = w1[0:KP, KP + half * KP // 2:KP + (half + 1) * KP // 2]
            nc.sync.dma_start(out=w1_half[half][:], in_=rows.rearrange("(p j) c -> p j c", j=PACK))
        nc.sync.dma_start(out=g1[:], in_=gain1.rearrange("(b p t) -> p b t", b=PASS2, t=PACK))
        for a in range(1, PASS1):
            load_w1(a, 1)
        nc.sync.dma_start(out=g2[:], in_=gain2.rearrange("(p t) -> p t", t=PACK))
        with nc.allow_non_contiguous_dma(reason="one cost value a partition"):
            nc.sync.dma_start(out=cost_t[:], in_=cost.rearrange("(m p) -> p m", p=P))
        nc.sync.dma_start(pos1_t[:], pos1)
        nc.sync.dma_start(pos2_t[:], pos2)

        w1_c, w1_s = {}, {}

        stage = [kept("stage%d" % c, [P, 2 * KP], F32) for c in range(NCH // 2)]

        def round_w1(a, b, u0, nu, eng, bf):
            dst = bf.rearrange("p (t m j) -> p m j t", t=2 * nu, j=PACK)
            src = w1_raw[a, b][:].rearrange("p j (m t) -> p m j t", t=PACK)[:, :, :, 2 * u0:2 * (u0 + nu)]
            if eng == "s":
                nc.scalar.copy(dst, src)
            else:
                nc.vector.tensor_copy(dst, src)

        def quant_w1(a, b, u0, nu, bf):
            c = kept("w1_c%d_%d_%d" % (a, b, u0), [P, nu * 2 * P], U32)
            s = kept("w1_s%d_%d_%d" % (a, b, u0), [P, nu * 2 * P], U8)
            for t in range(2 * nu):
                w1_c[a, b, 2 * u0 + t] = c[:, t * P:(t + 1) * P]
                w1_s[a, b, 2 * u0 + t] = s[:, t * P:(t + 1) * P]
            nc.vector.quantize_mx(out=c[:].bitcast(FP8X4), scales=s[:], in_=bf)

        v_w = {}

        def gather_v(a):
            v_w[a] = kept("v_w%d" % a, [P, S], U32, tag=("tab_w%d" % (a - 1) if a else None))
            nc.vector.tensor_copy(v_w[a][:], tab_w[a][:].bitcast(U32).indirect(offs_t[:]))

        gather_v(0)
        w2_c = kept("w2_c", [P, PASS2, 2 * H], U8)
        w2_s = kept("w2_s", [P, PASS2, H], U8)
        nc.vector.tensor_copy(
            w2_c[:].rearrange("p a (t m e) -> p a t m e", t=PACK, e=2),
            w2_raw[:].rearrange("p a (m t e) -> p a t m e", t=PACK, e=2),
        )
        nc.vector.tensor_copy(
            w2_s[:].rearrange("p a (t m) -> p a t m", t=PACK),
            w2_sraw[:].rearrange("p a (m t) -> p a t m", t=PACK),
        )
        v_s = kept("v_s", [P, S], U8)
        nc.vector.tensor_copy(v_s[:], tab_s[:].indirect(offs_t[:]))
        v2_s = kept("v2_s", [P, S2], U8)
        nc.vector.tensor_copy(v2_s[:], tab2_s[:].indirect(offs2_t[:]))

        z1 = {}

        def mm1(a, b, c):
            if a == 0:
                z1[b, c] = bank(c)
            cols = slice(c * CH, (c + 1) * CH)
            for t in range(PACK):
                nc.tensor.matmul_mx(
                    out=z1[b, c][:, t * CH:(t + 1) * CH],
                    lhsT=w1_c[a, b, t].bitcast(FP8X4),
                    lhsT_scale=w1_s[a, b, t],
                    rhs=v_w[a][:, cols].bitcast(FP8X4),
                    rhs_scale=v_s[4 * a:P, cols],
                    start=(a == 0 and t == 0),
                    stop=(a == PASS1 - 1 and t == PACK - 1),
                )

        act_bf = {}

        def staged(c, n):
            return stage[c // 2][:, (c % 2) * KP:(c % 2 + n) * KP].rearrange("p (n t) -> p n t", t=PACK)

        def activate(c, z, func):
            nc.scalar.activation(staged(c, 1), z[:].rearrange("p (t n) -> p n t", t=PACK), func, bias=zero[:])

        def apply_gain(key, c, n, gain_cols):
            bf = ring.tile([P, n * KP], BF16, name="act_bf", align_bytes=64)
            act_bf[key, c] = bf
            nc.vector.tensor_tensor(
                bf[:].rearrange("p (n t) -> p n t", t=PACK),
                staged(c, n),
                gain_cols.unsqueeze(1).to_broadcast([P, n * CH, PACK]),
                ALU.mult,
            )

        a_c = [kept("a_c%d" % b, [P, S], U32) for b in range(PASS2)]
        a_s = [kept("a_s%d" % b, [P, S], U8) for b in range(PASS2)]
        h_c = kept("h_c", [P, S], U32)
        h_s = kept("h_s", [P, S], U8)

        def quant(key, codes, scales, c, n):
            cols = slice(c * CH, (c + n) * CH)
            nc.vector.quantize_mx(out=codes[:, cols].bitcast(FP8X4), scales=scales[:, cols], in_=act_bf[key, c][:])

        def silu(b, c):
            activate(c, z1[b, c], ACT.Silu)

        def gain_a(b, c, n):
            apply_gain(b, c, n, g1[:, b, :])

        def quant_a(b, c, n):
            quant(b, a_c[b], a_s[b], c, n)

        def tanh(c):
            activate(c, z2[c], ACT.Tanh)

        def gain_h(c, n):
            apply_gain("h", c, n, g2[:, :])

        def quant_h(c, n):
            quant("h", h_c, h_s, c, n)

        z2 = {}

        def mm2(c):
            z2[c] = bank(c)
            cols = slice(c * CH, (c + 1) * CH)
            for b in range(PASS2):
                for t in range(PACK):
                    nc.tensor.matmul_mx(
                        out=z2[c][:, t * CH:(t + 1) * CH],
                        lhsT=w2_c[:, b, 2 * t * P:2 * (t + 1) * P].bitcast(FP4X4),
                        lhsT_scale=w2_s[:, b, t * P:(t + 1) * P],
                        rhs=a_c[b][:, cols].bitcast(FP8X4),
                        rhs_scale=a_s[b][:, cols],
                        start=(b == 0 and t == 0),
                        stop=(b == PASS2 - 1 and t == PACK - 1),
                    )

        for a in range(PASS1):
            if a:
                gather_v(a)
            bf = kept("w1_bf%d" % a, [P, 4 * KP], BF16, tag="tab_w%d" % a)
            if a < PASS1 - 1:
                round_w1(a, 0, 0, 2, "s", bf[:])
                quant_w1(a, 0, 0, 2, bf[:])
            else:
                round_w1(a, 0, 0, 1, "s", bf[:, 0:2 * KP])
                round_w1(a, 0, 1, 1, "v", bf[:, 2 * KP:4 * KP])
                quant_w1(a, 0, 1, 1, bf[:, 2 * KP:4 * KP])
                quant_w1(a, 0, 0, 1, bf[:, 0:2 * KP])
            for c in range(NCH):
                mm1(a, 0, c)

        def round_shared(a, holder):
            round_w1(a, 1, 0, 1, "s", holder[:, 0:KP].bitcast(BF16))
            round_w1(a, 1, 1, 1, "v", holder[:, KP:2 * KP].bitcast(BF16))

        bf01 = kept("w1_bf01", [P, 4 * KP], BF16, tag="tab_w2")
        for half in range(2):
            nc.vector.tensor_copy(
                bf01[:].rearrange("p (t m j) -> p m j t", t=PACK, j=PACK)[:, half * P // 2:(half + 1) * P // 2],
                w1_half[half][:].rearrange("p j (m t) -> p m j t", t=PACK),
            )
        silu(0, 0)
        gain_a(0, 0, 1)
        silu(0, 1)
        quant_w1(0, 1, 0, 2, bf01[:])
        gain_a(0, 1, 1)
        quant_a(0, 0, 1)
        round_shared(1, stage[0])
        quant_a(0, 1, 1)
        silu(0, 2)
        silu(0, 3)
        gain_a(0, 2, 2)
        quant_w1(1, 1, 0, 2, stage[0][:].bitcast(BF16))
        round_shared(2, stage[1])
        quant_a(0, 2, 2)
        quant_w1(2, 1, 0, 2, stage[1][:].bitcast(BF16))
        for c in (4, 6):
            silu(0, c)
            silu(0, c + 1)
            gain_a(0, c, 2)
        quant_a(0, 4, 2)

        tab2_w = kept("tab2_w", [P, T3], I32, tag="w1_raw2_1")
        nc.sync.dma_start(out=tab2_w[:], in_=tab2_words[0].rearrange("p t i -> p (t i)").bitcast(I32))
        v2_w = kept("v2_w", [P, S2], U32)
        e = [kept("e%d" % m, [P, S], F32) for m in range(MT)]

        def mm3(m, dst, lo, hi):
            rows = slice(m * P, (m + 1) * P)
            nc.tensor.matmul_mx(
                out=dst, lhsT=v2_w[:, rows].bitcast(FP8X4), lhsT_scale=v2_s[:, rows],
                rhs=h_c[:, lo:hi].bitcast(FP8X4), rhs_scale=h_s[:, lo:hi], start=True, stop=True,
            )

        eb = {}
        for c in range(0, NCH - 2, 2):
            for i in (c, c + 1):
                for a in range(PASS1):
                    mm1(a, 1, i)
                silu(1, i)
            gain_a(1, c, 2)
            if c == 0:
                quant_a(0, 6, 2)
            if c == 2:
                nc.vector.tensor_copy(v2_w[:], tab2_w[:].bitcast(U32).indirect(offs2_t[:]))
            if c >= 4:
                quant_h(c - 4, 2)
            if c >= 2:
                tanh(c - 2)
                tanh(c - 1)
            quant_a(1, c, 2)
            mm2(c)
            mm2(c + 1)
            if c >= 2:
                gain_h(c - 2, 2)
        for i in (6, 7):
            for a in range(PASS1):
                mm1(a, 1, i)
            silu(1, i)
            gain_a(1, i, 1)
            if i == 6:
                quant_h(2, 2)
        quant_a(1, 6, 1)
        mm2(6)
        tanh(4)
        tanh(5)
        quant_a(1, 7, 1)
        mm2(7)
        gain_h(4, 2)
        for m in range(MT):
            eb[m, 0] = bank(m)
            mm3(m, eb[m, 0][:], 0, 512)
        tanh(6)
        tanh(7)
        gain_h(6, 1)
        quant_h(4, 2)
        nc.scalar.copy(e[0][:, 0:512], eb[0, 0][:])
        gain_h(7, 1)
        quant_h(6, 1)
        quant_h(7, 1)
        eb[0, 1] = bank(4)
        mm3(0, eb[0, 1][:, 0:256], 512, 768)
        mm3(0, eb[0, 1][:, 256:384], 768, 896)
        nc.scalar.copy(e[0][:, 512:896], eb[0, 1][:, 0:384])
        eb[0, 2] = bank(5)
        mm3(0, eb[0, 2][:, 0:128], 896, 1024)
        nc.vector.tensor_copy(e[0][:, 896:1024], eb[0, 2][:, 0:128])
        for m, bk in ((1, 6), (2, 7), (3, 0)):
            eb[m, 1] = bank(bk)
            mm3(m, eb[m, 1][:], 512, 1024)

        half_cost = kept("half_cost", [P, MT], F32, tag="w1_raw1_1")
        nc.vector.tensor_scalar(half_cost[:], cost_t[:], 0.5, None, ALU.mult)

        before = {}

        def pick_before(m):
            before[m] = ring.tile([P, PAIRS], F32, name="before", align_bytes=64)
            nc.vector.tensor_copy(before[m][:], e[m][:].indirect(pos1_t[:]))

        def finish(m, lo, hi, last):
            n = hi - lo
            diff = ring.tile([P, n], F32, name="diff", align_bytes=64)
            th = ring.tile([P, n], F32, name="th", align_bytes=64)
            res = ring.tile([P, n], F32, name="res", align_bytes=64)
            nc.vector.tensor_tensor(
                diff[:], e[m][:].indirect(pos2_t[:, lo // 16:hi // 16]), before[m][:, lo:hi], ALU.subtract
            )
            nc.scalar.activation(th[:], diff[:], ACT.Tanh, bias=zero[:], scale=0.5)
            hc = half_cost[:, m:m + 1]
            if last:
                nc.vector.tensor_scalar(res[:], th[:], hc, hc, ALU.mult, ALU.add)
            else:
                nc.scalar.activation(res[:], th[:], ACT.Identity, bias=hc, scale=hc)
            nc.sync.dma_start(out=out[m * P:(m + 1) * P, lo:hi], in_=res[:])

        pick_before(0)
        for m in range(MT):
            if m + 1 < MT:
                nc.scalar.copy(e[m + 1][:, 0:512], eb[m + 1, 0][:])
                nc.scalar.copy(e[m + 1][:, 512:1024], eb[m + 1, 1][:])
                pick_before(m + 1)
                finish(m, 0, PAIRS, False)
            else:
                finish(m, 0, 384, True)
                finish(m, 384, PAIRS, True)
